import numpy as np
CORES = [401,273,145,17]
N = 4
ROOT = 1
def setup_inputs(rng):
    return {"x": rng.standard_normal((N, 128, N * 256), dtype=np.float32)}
def reference(x):
    return {"y": np.stack([x[ROOT][:, r * 256:(r + 1) * 256] for r in range(N)])}

@@ -1,0 +1,51 @@
+B = 256
+
+SCRATCH = {
+    "buf": ("sbuf", [128, 3 * B], "float32"),
+}
+SEMAPHORES = ["ld0", "ld1", "ld2", "arrived", "relay", "sent", "stored"]
+
+
+def slot(T, k):
+    return T.buf[:, k * B:(k + 1) * B]
+
+
+def rank_program(g, core, T, topo):
+    rank = T.rank_of(core)
+    if rank is None:
+        return
+    root = T.cores[T.root]
+    far = [c for c in T.cores if not topo.may_write(root, c)][0]
+    via = [c for c in T.cores if c != root and topo.same_plane(root, c)][0]
+
+    def send(dst, out_slot, in_slot, sem):
+        rid, pid = topo.addr(dst, core)
+        g.remote_dma(slot(T, out_slot), slot(T, in_slot), sem, T.sem.sent, pid, rid, topo.mask(core, dst))
+
+    def xblock(c):
+        r = T.rank_of(c)
+        return T.x[:, r * B:(r + 1) * B]
+
+    if core == root:
+        near = [c for c in T.cores if c not in (root, far, via)][0]
+        g.sync.dma_start(slot(T, 0), xblock(far)).then_inc(T.sem.ld0, 16)
+        g.scalar.dma_start(slot(T, 1), xblock(near)).then_inc(T.sem.ld1, 16)
+        g.sync.dma_start(slot(T, 2), xblock(via)).then_inc(T.sem.ld2, 16)
+        g.scalar.dma_start(T.y[:, :], xblock(root)).then_inc(T.sem.stored, 16)
+        g.wait_ge(T.sem.ld0, 16)
+        send(via, 1, 0, T.sem.relay)
+        g.wait_ge(T.sem.ld1, 16)
+        send(near, 0, 1, T.sem.arrived)
+        g.wait_ge(T.sem.ld2, 16)
+        send(via, 0, 2, T.sem.arrived)
+        g.wait_ge(T.sem.sent, 24)
+        g.wait_ge(T.sem.stored, 16)
+        return
+
+    g.sync.wait_ge(T.sem.arrived, 8)
+    g.sync.dma_start(T.y[:, :], slot(T, 0)).then_inc(T.sem.stored, 16)
+    if core == via:
+        g.wait_ge(T.sem.relay, 8)
+        send(far, 0, 1, T.sem.arrived)
+        g.wait_ge(T.sem.sent, 8)
+    g.wait_ge(T.sem.stored, 16)

@@ -1,13 +1,9 @@
 B = 256
 
 SCRATCH = {
-    "buf": ("sbuf", [128, 3 * B], "float32"),
+    "buf": ("dram", [3, 128, B], "float32"),
 }
 SEMAPHORES = ["ld0", "ld1", "ld2", "arrived", "relay", "sent", "stored"]
-
-
-def slot(T, k):
-    return T.buf[:, k * B:(k + 1) * B]
 
 
 def rank_program(g, core, T, topo):
@@ -20,7 +16,7 @@ def rank_program(g, core, T, topo):
 
     def send(dst, out_slot, in_slot, sem):
         rid, pid = topo.addr(dst, core)
-        g.remote_dma(slot(T, out_slot), slot(T, in_slot), sem, T.sem.sent, pid, rid, topo.mask(core, dst))
+        g.remote_dma(T.buf[out_slot], T.buf[in_slot], sem, T.sem.sent, pid, rid, topo.mask(core, dst))
 
     def xblock(c):
         r = T.rank_of(c)
@@ -28,9 +24,9 @@ def rank_program(g, core, T, topo):
 
     if core == root:
         near = [c for c in T.cores if c not in (root, far, via)][0]
-        g.sync.dma_start(slot(T, 0), xblock(far)).then_inc(T.sem.ld0, 16)
-        g.scalar.dma_start(slot(T, 1), xblock(near)).then_inc(T.sem.ld1, 16)
-        g.sync.dma_start(slot(T, 2), xblock(via)).then_inc(T.sem.ld2, 16)
+        g.sync.dma_start(T.buf[0], xblock(far)).then_inc(T.sem.ld0, 16)
+        g.scalar.dma_start(T.buf[1], xblock(near)).then_inc(T.sem.ld1, 16)
+        g.sync.dma_start(T.buf[2], xblock(via)).then_inc(T.sem.ld2, 16)
         g.scalar.dma_start(T.y[:, :], xblock(root)).then_inc(T.sem.stored, 16)
         g.wait_ge(T.sem.ld0, 16)
         send(via, 1, 0, T.sem.relay)
@@ -43,7 +39,7 @@ def rank_program(g, core, T, topo):
         return
 
     g.sync.wait_ge(T.sem.arrived, 8)
-    g.sync.dma_start(T.y[:, :], slot(T, 0)).then_inc(T.sem.stored, 16)
+    g.sync.dma_start(T.y[:, :], T.buf[0]).then_inc(T.sem.stored, 16)
     if core == via:
         g.wait_ge(T.sem.relay, 8)
         send(far, 0, 1, T.sem.arrived)

B = 256

SCRATCH = {
    "buf": ("dram", [3, 128, B], "float32"),
}
SEMAPHORES = ["ld0", "ld1", "ld2", "arrived", "relay", "sent", "stored"]


def rank_program(g, core, T, topo):
    rank = T.rank_of(core)
    if rank is None:
        return
    root = T.cores[T.root]
    far = [c for c in T.cores if not topo.may_write(root, c)][0]
    via = [c for c in T.cores if c != root and topo.same_plane(root, c)][0]

    def send(dst, out_slot, in_slot, sem):
        rid, pid = topo.addr(dst, core)
        g.remote_dma(T.buf[out_slot], T.buf[in_slot], sem, T.sem.sent, pid, rid, topo.mask(core, dst))

    def xblock(c):
        r = T.rank_of(c)
        return T.x[:, r * B:(r + 1) * B]

    if core == root:
        near = [c for c in T.cores if c not in (root, far, via)][0]
        g.sync.dma_start(T.buf[0], xblock(far)).then_inc(T.sem.ld0, 16)
        g.scalar.dma_start(T.buf[1], xblock(near)).then_inc(T.sem.ld1, 16)
        g.sync.dma_start(T.buf[2], xblock(via)).then_inc(T.sem.ld2, 16)
        g.scalar.dma_start(T.y[:, :], xblock(root)).then_inc(T.sem.stored, 16)
        g.wait_ge(T.sem.ld0, 16)
        send(via, 1, 0, T.sem.relay)
        g.wait_ge(T.sem.ld1, 16)
        send(near, 0, 1, T.sem.arrived)
        g.wait_ge(T.sem.ld2, 16)
        send(via, 0, 2, T.sem.arrived)
        g.wait_ge(T.sem.sent, 24)
        g.wait_ge(T.sem.stored, 16)
        return

    g.sync.wait_ge(T.sem.arrived, 8)
    g.sync.dma_start(T.y[:, :], T.buf[0]).then_inc(T.sem.stored, 16)
    if core == via:
        g.wait_ge(T.sem.relay, 8)
        send(far, 0, 1, T.sem.arrived)
        g.wait_ge(T.sem.sent, 8)
    g.wait_ge(T.sem.stored, 16)
